import numpy as np
import ml_dtypes


def mxq(x, axis, fmt="e4m3"):
    dtype, down = {"e4m3": (ml_dtypes.float8_e4m3fn, 7), "e5m2": (ml_dtypes.float8_e5m2, 14)}[fmt]
    v = np.moveaxis(np.asarray(x, np.float32).astype(ml_dtypes.bfloat16).astype(np.float64), axis, -1)
    blocks = v.reshape(v.shape[:-1] + (-1, 32))
    amax = np.abs(blocks).max(-1, keepdims=True)
    byte = np.maximum(np.where(amax > 0, np.frexp(amax)[1] - 1 + 127, 0) - down, 1)
    scale = np.exp2(byte - 127.0)
    codes = (blocks / scale).astype(np.float32).astype(dtype).astype(np.float64)
    return np.moveaxis((codes * scale).reshape(v.shape), -1, axis)


WIDE = False


def mx_kscale(k):
    if not WIDE:
        return np.ones(k)
    levels = np.array([10, -10, 5, -5, 0])
    if k % 512:
        return np.exp2(np.random.permutation(np.resize(levels, k // 32))).repeat(32)
    a = np.empty((k // 512, 16))
    for p in range(k // 512):
        a[p, :8] = np.random.permutation(np.resize(levels, 8))
        for g in range(8):
            far = levels[np.abs(levels - a[p, g]) >= 10]
            a[p, g + 8] = far[np.random.randint(len(far))]
    return np.exp2(a.ravel()).repeat(32)


def f64(x):
    return np.asarray(x).astype(np.float64)


def striped(idx):
    return np.tile(idx.reshape(-1, 16).T, (8, 1)).astype(np.uint16)


def unstriped(offs):
    return offs[:16].T.reshape(-1).astype(np.int64)


def pack_weight(w):
    k, n = w.shape
    w = f64(np.asarray(w, np.float32).astype(ml_dtypes.bfloat16)).reshape(k // 32, 32, n)
    amax = np.abs(w).max(1)
    byte = np.clip(np.where(amax > 0, np.frexp(amax)[1] - 1 + 127 - 7, 1), 1, 254)
    scaled = (w * np.exp2(127.0 - byte)[:, None, :]).reshape(k, n).astype(np.float32)
    words = np.ascontiguousarray(scaled.reshape(k // 512, 128, 4, n).transpose(0, 1, 3, 2)).astype(ml_dtypes.float8_e4m3fn).view(np.uint8)
    return words, np.ascontiguousarray(byte.astype(np.uint8).reshape(k // 512, 16, n))


def unpack_weight(words, scales):
    g, p, n, _ = words.shape
    vals = np.ascontiguousarray(words).view(ml_dtypes.float8_e4m3fn).astype(np.float64) * np.repeat(np.exp2(scales.astype(np.float64) - 127.0), 8, axis=1)[..., None]
    return vals.transpose(0, 1, 3, 2).reshape(g * 512, n)


K, T, S, N, D = 1024, 1024, 512, 256, 3
P = 2 ** 7


def setup_inputs():
    n = np.random.standard_normal
    s = mx_kscale(K)[:, None]
    packed_xT = pack_weight(n((K, T)) * s)
    return {
        "x_words": packed_xT[0],
        "x_scales": packed_xT[1],
        "w1": (n((K, N)) / np.sqrt(K) / s).astype(np.float32),
        "gain": (np.tile(np.random.uniform(0.05, 0.5, (D, 1, S)), (1, P, 1))).astype(np.float32),
        "owng": (np.tile(np.random.uniform(0.6, 1.6, S), (P, 1))).astype(np.float32),
        "goal": (np.random.uniform(0.4, 1.2, (N, 1))).astype(np.float32),
        "cap": (np.tile(np.random.uniform(0.5, 1.5, S), (P, 1))).astype(np.float32),
        "offs": striped(np.random.permutation(T)[:S]),
        "pos1": striped(np.random.permutation(S)[:S]),
        "pos2": striped(np.random.permutation(S)[:S]),
        "pos3": striped(np.random.permutation(S)[:S]),
    }


def reference(x_words, x_scales, w1, gain, owng, goal, cap, offs, pos1, pos2, pos3):
    xq = unpack_weight(x_words, x_scales)[:, unstriped(offs)]
    y = mxq(f64(w1), 0, "e4m3").T @ xq
    pw = np.exp(0.4 * y)
    ia = pw[:, unstriped(pos1)] * f64(gain)[0, :1] + pw[:, unstriped(pos2)] * f64(gain)[1, :1] + pw[:, unstriped(pos3)] * f64(gain)[2, :1] + 0.1
    pn = np.minimum(f64(goal) * (ia / f64(owng)[:1]), f64(cap)[:1])
    ib = pn[:, unstriped(pos1)] * f64(gain)[0, :1] + pn[:, unstriped(pos2)] * f64(gain)[1, :1] + pn[:, unstriped(pos3)] * f64(gain)[2, :1] + 0.1
    return np.log((f64(owng)[:1] * pn) / ib + 1.0)

@@ -1,0 +1,262 @@
+from contextlib import ExitStack
+
+import concourse.mybir as mybir
+from concourse.masks import make_identity
+
+K, T, S, N, D = 1024, 1024, 512, 256, 3
+FLOPS = 2 * K * S * N
+
+F32 = mybir.dt.float32
+BF16 = mybir.dt.bfloat16
+I32 = mybir.dt.int32
+U32 = mybir.dt.uint32
+U16 = mybir.dt.uint16
+U8 = mybir.dt.uint8
+FP8X4 = mybir.dt.float8_e4m3fn_x4
+ACT = mybir.ActivationFunctionType
+ALU = mybir.AluOpType
+
+P = 128
+PACK = 4
+PASSES = K // (P * PACK)
+BLOCKS = N // P
+CHUNKS = S // P
+HALF = S // 2
+LIST = 16
+WINDOW = S + 16
+NOISE = 0.1
+OWN_ROW, GAIN_ROW, ROWS = 0, 4, 8
+WIDE = 2048
+OFFLOAD = (1,)
+
+
+def tile_picked_yfosch_rate_p_kernel(
+    tc, x_words, x_scales, w1, gain, owng, goal, cap, offs, pos1, pos2, pos3, out
+):
+    nc = tc.nc
+    with ExitStack() as ctx:
+        lists = ctx.enter_context(tc.tile_pool(name="lists", bufs=1))
+        keep = ctx.enter_context(tc.tile_pool(name="keep", bufs=1))
+        psum = ctx.enter_context(tc.psum_pool(name="psum", bufs=1))
+
+        def sb(shape, dtype, name):
+            return keep.tile(shape, dtype, name=name, align_bytes=64)
+
+        banks = [psum.tile([P, S], F32, name=f"bank{i}") for i in range(8)]
+
+        picked = lists.tile([P, S // LIST], U16, name="picked")
+        places = [lists.tile([P, S // LIST], U16, name=f"places{d}") for d in range(D)]
+
+        table_scales = sb([P, T], U8, "table_scales")
+        table_words = [sb([P, T], U32, f"table_words{o}") for o in range(PASSES)]
+        w_raw = [sb([P, PACK, N], F32, f"w_raw{o}") for o in range(PASSES)]
+        exponents = sb([P, WIDE], F32, "exponents")
+        gains = [sb([P, S], F32, f"gains{d}") for d in range(D)]
+        caps = sb([P, S], F32, "caps")
+        rows = sb([P, P], F32, "rows")
+        ident = sb([P, P], F32, "ident")
+        first = [sb([P, WINDOW], F32, f"first{b}") for b in range(BLOCKS)]
+        power = [sb([P, WINDOW], F32, f"power{b}") for b in range(BLOCKS)]
+
+        def load_words(o):
+            nc.sync.dma_start(
+                out=table_words[o][:].bitcast(I32),
+                in_=x_words[o].rearrange("p n t -> p (n t)").bitcast(I32),
+            )
+
+        def load_w(o):
+            k_rows = w1[o * P * PACK : (o + 1) * P * PACK, :]
+            nc.sync.dma_start(out=w_raw[o][:], in_=k_rows.rearrange("(p t) m -> p t m", t=PACK))
+
+        nc.vector.memset(table_scales[:].bitcast(I32), 0)
+        nc.vector.memset(rows[:], 0.0)
+        nc.vector.memset(exponents[:, S:], 0.0)
+        nc.sync.dma_start(out=picked[:], in_=offs)
+        for q in range(4):
+            nc.sync.dma_start(
+                out=table_scales[32 * q : 32 * q + 8, :].bitcast(I32),
+                in_=x_scales[:, 4 * q : 4 * q + 4, :].bitcast(I32),
+            )
+        load_words(0)
+        load_w(0)
+        load_w(1)
+        for place, pos in zip(places, (pos1, pos2, pos3)):
+            nc.sync.dma_start(out=place[:], in_=pos)
+        nc.sync.dma_start(
+            out=rows[GAIN_ROW : GAIN_ROW + CHUNKS, :], in_=gain[D - 1, 0].rearrange("(c n) -> c n", n=P)
+        )
+        nc.sync.dma_start(
+            out=rows[OWN_ROW : OWN_ROW + CHUNKS, :], in_=owng[0].rearrange("(c n) -> c n", n=P)
+        )
+        load_words(1)
+        for d in range(D):
+            nc.sync.dma_start(out=gains[d][:], in_=gain[d])
+        nc.sync.dma_start(out=caps[:], in_=cap)
+        goals = sb([P, BLOCKS], F32, "goals")
+        with nc.allow_non_contiguous_dma(reason="one goal a partition and block"):
+            nc.sync.dma_start(out=goals[:], in_=goal.rearrange("(b p) o -> p (b o)", p=P))
+
+        make_identity(nc, ident[:])
+        for window in first + power:
+            nc.gpsimd.memset(window[:, S:], 0.0)
+
+        warm = sb([P, 1], F32, "warm")
+        warm2 = sb([P, 1], F32, "warm2")
+        nc.vector.memset(warm[:], 0.0)
+        nc.scalar.activation(warm2[:], warm[:], ACT.Exp)
+
+        scales = sb([P, S], U8, "scales")
+        words = [sb([P, S], U32, f"words{o}") for o in range(PASSES)]
+        w_bf = [sb([P, N, PACK], BF16, f"w_bf{o}") for o in range(PASSES)]
+        w_codes = [sb([P, N], U32, f"w_codes{o}") for o in range(PASSES)]
+        w_scales = [sb([P, N], U8, f"w_scales{o}") for o in range(PASSES)]
+
+        def entries(a, z):
+            return slice(a // LIST, z // LIST)
+
+        def chunk(c):
+            return slice(c * P, (c + 1) * P)
+
+        def cast_w(copy, b, o):
+            copy(w_bf[o][:, chunk(b), :], w_raw[o][:, :, chunk(b)].rearrange("p t m -> p m t"))
+
+        def quantize_w(o):
+            nc.vector.quantize_mx(
+                out=w_codes[o][:].bitcast(FP8X4),
+                scales=w_scales[o][:],
+                in_=w_bf[o][:].rearrange("p m t -> p (m t)"),
+            )
+
+        def product(acc, b, o, a, z):
+            nc.tensor.matmul_mx(
+                out=acc,
+                lhsT=w_codes[o][:, chunk(b)].bitcast(FP8X4),
+                lhsT_scale=w_scales[o][:, chunk(b)],
+                rhs=words[o][:, a:z].bitcast(FP8X4),
+                rhs_scale=scales[4 * o :, a:z],
+                start=(o == 0),
+                stop=(o == PASSES - 1),
+            )
+
+        def turn(dst, src, start, stop):
+            nc.tensor.matmul(dst, lhsT=src, rhs=ident[:], is_transpose=True, start=start, stop=stop)
+
+        nc.vector.tensor_copy(scales[:], table_scales[:].indirect(picked[:]))
+        nc.vector.tensor_copy(words[0][:], table_words[0][:].indirect(picked[:]))
+        cast_w(nc.scalar.copy, 0, 0)
+        cast_w(nc.scalar.copy, 1, 0)
+        quantize_w(0)
+        cast_w(nc.scalar.copy, 0, 1)
+        cast_w(nc.vector.tensor_copy, 1, 1)
+        quantize_w(1)
+        for h in range(2):
+            product(banks[h][:, :HALF], 0, 0, h * HALF, (h + 1) * HALF)
+        product(banks[2][:], 1, 0, 0, S)
+        for h in range(2):
+            a, z = h * HALF, (h + 1) * HALF
+            nc.vector.tensor_copy(words[1][:, a:z], table_words[1][:].indirect(picked[:, entries(a, z)]))
+            product(banks[h][:, :HALF], 0, 1, a, z)
+            nc.scalar.activation(first[0][:, a:z], banks[h][:, :HALF], ACT.Exp, scale=0.4)
+            if 0 in OFFLOAD:
+                nc.scalar.copy(exponents[:, a:z], banks[h][:, :HALF])
+        product(banks[2][:], 1, 1, 0, S)
+        turn(banks[0][:, HALF : HALF + P], rows[:], True, True)
+        cols = sb([P, ROWS], F32, "cols")
+        inv_own = sb([P, CHUNKS], F32, "inv_own")
+        floor = sb([P, CHUNKS], F32, "floor")
+        last_gain = sb([P, CHUNKS], F32, "last_gain")
+        nc.scalar.copy(cols[:], banks[0][:, HALF : HALF + ROWS])
+        nc.vector.reciprocal(inv_own[:], cols[:, OWN_ROW : OWN_ROW + CHUNKS])
+        nc.gpsimd.tensor_scalar_mul(floor[:], inv_own[:], NOISE)
+        nc.gpsimd.tensor_tensor(last_gain[:], inv_own[:], cols[:, GAIN_ROW : GAIN_ROW + CHUNKS], ALU.mult)
+
+
+        def heard(window, name, a, z, bank, terms):
+            count = (z - a) // P
+            for d in range(terms):
+                term = sb([P, z - a], F32, f"{name}{d}")
+                index = places[d][:] if z - a == S else places[d][:, entries(a, z)]
+                nc.vector.tensor_tensor(term[:], window[:].indirect(index), gains[d][:, a:z], ALU.mult)
+                for c in range(count):
+                    turn(bank[:, chunk(c)], term[:, chunk(c)], d == 0 and c == 0, d == terms - 1 and c == count - 1)
+
+        def heard_last(b, turned, back):
+            term = sb([P, S], F32, f"last{b}")
+            nc.scalar.activation(term[:], exponents[:].indirect(places[D - 1][:]), ACT.Exp, scale=0.4)
+            if b == BLOCKS - 1:
+                warm3 = sb([P, 1], F32, "warm3")
+                nc.scalar.activation(warm3[:], term[:, 0:1], ACT.Ln)
+            for c in range(CHUNKS):
+                turn(turned[:, chunk(c)], term[:, chunk(c)], True, True)
+            weighted = sb([P, S], F32, f"weighted{b}")
+            for c in range(CHUNKS):
+                nc.scalar.activation(
+                    weighted[:, chunk(c)], turned[:, chunk(c)], ACT.Copy, scale=last_gain[:, c : c + 1]
+                )
+            for c in range(CHUNKS):
+                turn(back[:, chunk(c)], weighted[:, chunk(c)], c == 0, False)
+
+        def wanted(b, turned, back):
+            ratio = sb([P, S], F32, f"ratio{b}")
+            for c in range(CHUNKS):
+                nc.scalar.activation(
+                    ratio[:, chunk(c)], turned[:, chunk(c)], ACT.Identity,
+                    scale=inv_own[:, c : c + 1], bias=floor[:, c : c + 1],
+                )
+            for c in range(CHUNKS):
+                turn(back[:, chunk(c)], ratio[:, chunk(c)], c == 0 and b not in OFFLOAD, c == CHUNKS - 1)
+
+        def limit(b, back, bank):
+            nc.vector.scalar_tensor_tensor(
+                power[b][:, :S], back[:], goals[:, b : b + 1], caps[:], ALU.mult, ALU.min
+            )
+            for c in range(CHUNKS):
+                turn(bank[:, chunk(c)], power[b][:, chunk(c)], True, True)
+            signal = sb([P, S], F32, f"signal{b}")
+            for c in range(CHUNKS):
+                nc.scalar.activation(
+                    signal[:, chunk(c)], bank[:, chunk(c)], ACT.Copy, scale=cols[:, OWN_ROW + c : OWN_ROW + c + 1]
+                )
+            return signal
+
+        def rate_logs(b, signal, a, z, turned, both):
+            width = z - a
+            count = width // P
+            noisy = sb([P, width], F32, f"noisy{b}_{a}")
+            nc.scalar.activation(noisy[:], turned[:, :width], ACT.Copy, bias=NOISE)
+            for c in range(count):
+                turn(both[:, chunk(count + c)], signal[:, a + c * P : a + (c + 1) * P], c == 0, False)
+            for c in range(count):
+                turn(both[:, chunk(c)], noisy[:, chunk(c)], False, False)
+                turn(both[:, chunk(count + c)], noisy[:, chunk(c)], False, c == count - 1)
+            logs = sb([P, 2 * width], F32, f"logs{b}_{a}")
+            nc.scalar.activation(logs[:], both[:, : 2 * width], ACT.Ln)
+            return logs
+
+        def finish(b, logs, a, z):
+            width = z - a
+            rate = sb([P, width], F32, f"rate{b}_{a}")
+            nc.vector.tensor_tensor(rate[:], logs[:, width:], logs[:, :width], ALU.subtract)
+            nc.sync.dma_start(out=out[b * P : (b + 1) * P, a:z], in_=rate[:])
+
+        nc.scalar.activation(first[1][:, :S], banks[2][:], ACT.Exp, scale=0.4)
+        nc.scalar.copy(exponents[:, :S], banks[2][:])
+        heard(first[0], "t00", 0, S, banks[3], D)
+        wanted(0, banks[3], banks[5])
+        heard_last(1, banks[4], banks[6])
+        heard(first[1], "t01", 0, S, banks[3], D - 1)
+        wanted(1, banks[3], banks[6])
+        signals = [limit(0, banks[5], banks[0])]
+        pieces = [(0, 0, HALF), (0, HALF, S), (1, 0, HALF), (1, HALF, HALF + P), (1, HALF + P, S)]
+        turned_banks = [banks[3], banks[4]]
+        both_banks = [banks[7], banks[2], banks[5]]
+        pending = []
+        for i, (b, a, z) in enumerate(pieces):
+            heard(power[b], f"t1{b}_{a}_", a, z, turned_banks[i % 2], D)
+            if i == 1:
+                signals.append(limit(1, banks[6], banks[1]))
+            if len(pending) == 2:
+                finish(*pending.pop(0))
+            pending.append((b, rate_logs(b, signals[b], a, z, turned_banks[i % 2], both_banks[i % 3]), a, z))
+        for job in pending:
+            finish(*job)

@@ -49,7 +49,7 @@ def tile_picked_yfosch_rate_p_kernel(
 
         table_scales = sb([P, T], U8, "table_scales")
         table_words = [sb([P, T], U32, f"table_words{o}") for o in range(PASSES)]
-        w_raw = [sb([P, PACK, N], F32, f"w_raw{o}") for o in range(PASSES)]
+        w_raw = [[sb([P, PACK, P], F32, f"w_raw{b}{o}") for o in range(PASSES)] for b in range(BLOCKS)]
         exponents = sb([P, WIDE], F32, "exponents")
         gains = [sb([P, S], F32, f"gains{d}") for d in range(D)]
         caps = sb([P, S], F32, "caps")
@@ -64,34 +64,38 @@ def tile_picked_yfosch_rate_p_kernel(
                 in_=x_words[o].rearrange("p n t -> p (n t)").bitcast(I32),
             )
 
-        def load_w(o):
-            k_rows = w1[o * P * PACK : (o + 1) * P * PACK, :]
-            nc.sync.dma_start(out=w_raw[o][:], in_=k_rows.rearrange("(p t) m -> p t m", t=PACK))
+        def load_w(b, o):
+            k_rows = w1[o * P * PACK : (o + 1) * P * PACK, b * P : (b + 1) * P]
+            nc.sync.dma_start(out=w_raw[b][o][:], in_=k_rows.rearrange("(p t) m -> p t m", t=PACK))
 
         nc.vector.memset(table_scales[:].bitcast(I32), 0)
+        warm = sb([P, 1], F32, "warm")
+        nc.vector.memset(warm[:], 0.0)
         nc.vector.memset(rows[:], 0.0)
         nc.vector.memset(exponents[:, S:], 0.0)
         nc.sync.dma_start(out=picked[:], in_=offs)
+        load_words(0)
         for q in range(4):
             nc.sync.dma_start(
                 out=table_scales[32 * q : 32 * q + 8, :].bitcast(I32),
                 in_=x_scales[:, 4 * q : 4 * q + 4, :].bitcast(I32),
             )
-        load_words(0)
-        load_w(0)
-        load_w(1)
-        for place, pos in zip(places, (pos1, pos2, pos3)):
-            nc.sync.dma_start(out=place[:], in_=pos)
-        nc.sync.dma_start(
-            out=rows[GAIN_ROW : GAIN_ROW + CHUNKS, :], in_=gain[D - 1, 0].rearrange("(c n) -> c n", n=P)
-        )
-        nc.sync.dma_start(
-            out=rows[OWN_ROW : OWN_ROW + CHUNKS, :], in_=owng[0].rearrange("(c n) -> c n", n=P)
-        )
+        load_w(0, 0)
+        load_w(0, 1)
+        nc.sync.dma_start(out=rows[GAIN_ROW : GAIN_ROW + CHUNKS, :], in_=gain[D - 1, 0].rearrange("(c n) -> c n", n=P))
+        nc.sync.dma_start(out=rows[OWN_ROW : OWN_ROW + CHUNKS, :], in_=owng[0].rearrange("(c n) -> c n", n=P))
         load_words(1)
-        for d in range(D):
-            nc.sync.dma_start(out=gains[d][:], in_=gain[d])
+        nc.sync.dma_start(out=places[0][:], in_=pos1)
+        nc.sync.dma_start(out=places[1][:], in_=pos2)
+        nc.sync.dma_start(out=places[2][:], in_=pos3)
+        load_w(1, 0)
+        load_w(1, 1)
+        nc.sync.dma_start(out=gains[0][:], in_=gain[0])
+        nc.sync.dma_start(out=gains[1][:], in_=gain[1])
+        nc.sync.dma_start(out=gains[2][:], in_=gain[2])
         nc.sync.dma_start(out=caps[:], in_=cap)
+        own_tail = sb([P, P], F32, "own_tail")
+        nc.sync.dma_start(out=own_tail[:], in_=owng[:, S - P :])
         goals = sb([P, BLOCKS], F32, "goals")
         with nc.allow_non_contiguous_dma(reason="one goal a partition and block"):
             nc.sync.dma_start(out=goals[:], in_=goal.rearrange("(b p) o -> p (b o)", p=P))
@@ -100,16 +104,14 @@ def tile_picked_yfosch_rate_p_kernel(
         for window in first + power:
             nc.gpsimd.memset(window[:, S:], 0.0)
 
-        warm = sb([P, 1], F32, "warm")
         warm2 = sb([P, 1], F32, "warm2")
-        nc.vector.memset(warm[:], 0.0)
         nc.scalar.activation(warm2[:], warm[:], ACT.Exp)
 
         scales = sb([P, S], U8, "scales")
         words = [sb([P, S], U32, f"words{o}") for o in range(PASSES)]
-        w_bf = [sb([P, N, PACK], BF16, f"w_bf{o}") for o in range(PASSES)]
-        w_codes = [sb([P, N], U32, f"w_codes{o}") for o in range(PASSES)]
-        w_scales = [sb([P, N], U8, f"w_scales{o}") for o in range(PASSES)]
+        w_bf = [sb([P, PASSES, P, PACK], BF16, f"w_bf{b}") for b in range(BLOCKS)]
+        w_codes = [sb([P, PASSES, P], U32, f"w_codes{b}") for b in range(BLOCKS)]
+        w_scales = [sb([P, PASSES, P], U8, f"w_scales{b}") for b in range(BLOCKS)]
 
         def entries(a, z):
             return slice(a // LIST, z // LIST)
@@ -118,20 +120,20 @@ def tile_picked_yfosch_rate_p_kernel(
             return slice(c * P, (c + 1) * P)
 
         def cast_w(copy, b, o):
-            copy(w_bf[o][:, chunk(b), :], w_raw[o][:, :, chunk(b)].rearrange("p t m -> p m t"))
+            copy(w_bf[b][:, o], w_raw[b][o][:].rearrange("p t m -> p m t"))
 
-        def quantize_w(o):
+        def quantize_w(b):
             nc.vector.quantize_mx(
-                out=w_codes[o][:].bitcast(FP8X4),
-                scales=w_scales[o][:],
-                in_=w_bf[o][:].rearrange("p m t -> p (m t)"),
+                out=w_codes[b][:].rearrange("p o m -> p (o m)").bitcast(FP8X4),
+                scales=w_scales[b][:].rearrange("p o m -> p (o m)"),
+                in_=w_bf[b][:].rearrange("p o m t -> p (o m t)"),
             )
 
         def product(acc, b, o, a, z):
             nc.tensor.matmul_mx(
                 out=acc,
-                lhsT=w_codes[o][:, chunk(b)].bitcast(FP8X4),
-                lhsT_scale=w_scales[o][:, chunk(b)],
+                lhsT=w_codes[b][:, o].bitcast(FP8X4),
+                lhsT_scale=w_scales[b][:, o],
                 rhs=words[o][:, a:z].bitcast(FP8X4),
                 rhs_scale=scales[4 * o :, a:z],
                 start=(o == 0),
@@ -141,122 +143,130 @@ def tile_picked_yfosch_rate_p_kernel(
         def turn(dst, src, start, stop):
             nc.tensor.matmul(dst, lhsT=src, rhs=ident[:], is_transpose=True, start=start, stop=stop)
 
-        nc.vector.tensor_copy(scales[:], table_scales[:].indirect(picked[:]))
         nc.vector.tensor_copy(words[0][:], table_words[0][:].indirect(picked[:]))
+        nc.vector.tensor_copy(scales[:], table_scales[:].indirect(picked[:]))
         cast_w(nc.scalar.copy, 0, 0)
-        cast_w(nc.scalar.copy, 1, 0)
-        quantize_w(0)
         cast_w(nc.scalar.copy, 0, 1)
-        cast_w(nc.vector.tensor_copy, 1, 1)
-        quantize_w(1)
-        for h in range(2):
-            product(banks[h][:, :HALF], 0, 0, h * HALF, (h + 1) * HALF)
-        product(banks[2][:], 1, 0, 0, S)
-        for h in range(2):
-            a, z = h * HALF, (h + 1) * HALF
-            nc.vector.tensor_copy(words[1][:, a:z], table_words[1][:].indirect(picked[:, entries(a, z)]))
-            product(banks[h][:, :HALF], 0, 1, a, z)
-            nc.scalar.activation(first[0][:, a:z], banks[h][:, :HALF], ACT.Exp, scale=0.4)
-            if 0 in OFFLOAD:
-                nc.scalar.copy(exponents[:, a:z], banks[h][:, :HALF])
-        product(banks[2][:], 1, 1, 0, S)
-        turn(banks[0][:, HALF : HALF + P], rows[:], True, True)
+        quantize_w(0)
+        turn(banks[6][:, :P], rows[:], True, True)
         cols = sb([P, ROWS], F32, "cols")
         inv_own = sb([P, CHUNKS], F32, "inv_own")
         floor = sb([P, CHUNKS], F32, "floor")
         last_gain = sb([P, CHUNKS], F32, "last_gain")
-        nc.scalar.copy(cols[:], banks[0][:, HALF : HALF + ROWS])
+        nc.scalar.copy(cols[:], banks[6][:, :ROWS])
         nc.vector.reciprocal(inv_own[:], cols[:, OWN_ROW : OWN_ROW + CHUNKS])
         nc.gpsimd.tensor_scalar_mul(floor[:], inv_own[:], NOISE)
         nc.gpsimd.tensor_tensor(last_gain[:], inv_own[:], cols[:, GAIN_ROW : GAIN_ROW + CHUNKS], ALU.mult)
+        spans = [(0, HALF), (HALF, HALF + P), (HALF + P, S)]
+        span_banks = [banks[0], banks[1], banks[7]]
+        for bank, (a, z) in zip(span_banks, spans):
+            product(bank[:, : z - a], 0, 0, a, z)
+        for bank, (a, z) in zip(span_banks, spans):
+            nc.vector.tensor_copy(words[1][:, a:z], table_words[1][:].indirect(picked[:, entries(a, z)]))
+            product(bank[:, : z - a], 0, 1, a, z)
+            nc.scalar.activation(first[0][:, a:z], bank[:, : z - a], ACT.Exp, scale=0.4)
+        cast_w(nc.vector.tensor_copy, 1, 0)
+        cast_w(nc.vector.tensor_copy, 1, 1)
+        quantize_w(1)
+        product(banks[2][:], 1, 0, 0, S)
+        product(banks[2][:], 1, 1, 0, S)
+        def gather(window, d, a, z, term):
+            index = places[d][:] if z - a == S else places[d][:, entries(a, z)]
+            nc.vector.tensor_tensor(term, window[:].indirect(index), gains[d][:, a:z], ALU.mult)
 
+        def add_turned(turned, term, start, stop):
+            count = term.shape[1] // P
+            for c in range(count):
+                turn(turned[:, chunk(c)], term[:, chunk(c)], start and c == 0, stop and c == count - 1)
 
-        def heard(window, name, a, z, bank, terms):
-            count = (z - a) // P
-            for d in range(terms):
-                term = sb([P, z - a], F32, f"{name}{d}")
-                index = places[d][:] if z - a == S else places[d][:, entries(a, z)]
-                nc.vector.tensor_tensor(term[:], window[:].indirect(index), gains[d][:, a:z], ALU.mult)
-                for c in range(count):
-                    turn(bank[:, chunk(c)], term[:, chunk(c)], d == 0 and c == 0, d == terms - 1 and c == count - 1)
+        def per_own_gain(ratio, turned, a):
+            for c in range(ratio.shape[1] // P):
+                link = slice(a // P + c, a // P + c + 1)
+                nc.scalar.activation(
+                    ratio[:, chunk(c)], turned[:, chunk(c)], ACT.Identity, scale=inv_own[:, link], bias=floor[:, link]
+                )
 
-        def heard_last(b, turned, back):
-            term = sb([P, S], F32, f"last{b}")
-            nc.scalar.activation(term[:], exponents[:].indirect(places[D - 1][:]), ACT.Exp, scale=0.4)
-            if b == BLOCKS - 1:
+        def limit(b, back, a, z):
+            nc.vector.scalar_tensor_tensor(power[b][:, a:z], back, goals[:, b : b + 1], caps[:, a:z], ALU.mult, ALU.min)
+
+        def heard_last(b, turned):
+            last = sb([P, S], F32, f"last{b}")
+            nc.scalar.activation(last[:], exponents[:].indirect(places[D - 1][:]), ACT.Exp, scale=0.4)
+            if b == 1:
                 warm3 = sb([P, 1], F32, "warm3")
-                nc.scalar.activation(warm3[:], term[:, 0:1], ACT.Ln)
-            for c in range(CHUNKS):
-                turn(turned[:, chunk(c)], term[:, chunk(c)], True, True)
+                nc.scalar.activation(warm3[:], last[:, 0:1], ACT.Ln)
+            add_turned(turned, last[:], True, True)
             weighted = sb([P, S], F32, f"weighted{b}")
             for c in range(CHUNKS):
-                nc.scalar.activation(
-                    weighted[:, chunk(c)], turned[:, chunk(c)], ACT.Copy, scale=last_gain[:, c : c + 1]
-                )
-            for c in range(CHUNKS):
-                turn(back[:, chunk(c)], weighted[:, chunk(c)], c == 0, False)
+                nc.scalar.activation(weighted[:, chunk(c)], turned[:, chunk(c)], ACT.Copy, scale=last_gain[:, c : c + 1])
+            return weighted
 
-        def wanted(b, turned, back):
-            ratio = sb([P, S], F32, f"ratio{b}")
-            for c in range(CHUNKS):
-                nc.scalar.activation(
-                    ratio[:, chunk(c)], turned[:, chunk(c)], ACT.Identity,
-                    scale=inv_own[:, c : c + 1], bias=floor[:, c : c + 1],
-                )
-            for c in range(CHUNKS):
-                turn(back[:, chunk(c)], ratio[:, chunk(c)], c == 0 and b not in OFFLOAD, c == CHUNKS - 1)
-
-        def limit(b, back, bank):
-            nc.vector.scalar_tensor_tensor(
-                power[b][:, :S], back[:], goals[:, b : b + 1], caps[:], ALU.mult, ALU.min
-            )
-            for c in range(CHUNKS):
-                turn(bank[:, chunk(c)], power[b][:, chunk(c)], True, True)
-            signal = sb([P, S], F32, f"signal{b}")
-            for c in range(CHUNKS):
-                nc.scalar.activation(
-                    signal[:, chunk(c)], bank[:, chunk(c)], ACT.Copy, scale=cols[:, OWN_ROW + c : OWN_ROW + c + 1]
-                )
-            return signal
-
-        def rate_logs(b, signal, a, z, turned, both):
-            width = z - a
-            count = width // P
-            noisy = sb([P, width], F32, f"noisy{b}_{a}")
-            nc.scalar.activation(noisy[:], turned[:, :width], ACT.Copy, bias=NOISE)
-            for c in range(count):
-                turn(both[:, chunk(count + c)], signal[:, a + c * P : a + (c + 1) * P], c == 0, False)
-            for c in range(count):
-                turn(both[:, chunk(c)], noisy[:, chunk(c)], False, False)
-                turn(both[:, chunk(count + c)], noisy[:, chunk(c)], False, c == count - 1)
-            logs = sb([P, 2 * width], F32, f"logs{b}_{a}")
-            nc.scalar.activation(logs[:], both[:, : 2 * width], ACT.Ln)
-            return logs
-
-        def finish(b, logs, a, z):
-            width = z - a
-            rate = sb([P, width], F32, f"rate{b}_{a}")
-            nc.vector.tensor_tensor(rate[:], logs[:, width:], logs[:, :width], ALU.subtract)
-            nc.sync.dma_start(out=out[b * P : (b + 1) * P, a:z], in_=rate[:])
-
+        halves = [(0, HALF), (HALF, S)]
+        ratio = sb([P, S], F32, "ratio0")
         nc.scalar.activation(first[1][:, :S], banks[2][:], ACT.Exp, scale=0.4)
         nc.scalar.copy(exponents[:, :S], banks[2][:])
-        heard(first[0], "t00", 0, S, banks[3], D)
-        wanted(0, banks[3], banks[5])
-        heard_last(1, banks[4], banks[6])
-        heard(first[1], "t01", 0, S, banks[3], D - 1)
-        wanted(1, banks[3], banks[6])
-        signals = [limit(0, banks[5], banks[0])]
-        pieces = [(0, 0, HALF), (0, HALF, S), (1, 0, HALF), (1, HALF, HALF + P), (1, HALF + P, S)]
-        turned_banks = [banks[3], banks[4]]
-        both_banks = [banks[7], banks[2], banks[5]]
-        pending = []
+        terms = [sb([P, S], F32, f"term0{d}") for d in range(D)]
+        for d in range(D - 1):
+            gather(first[0], d, 0, S, terms[d][:])
+            for h, (a, z) in enumerate(halves):
+                add_turned(banks[3 + h], terms[d][:, a:z], d == 0, False)
+        for h, (a, z) in enumerate(halves):
+            gather(first[0], D - 1, a, z, terms[D - 1][:, a:z])
+            add_turned(banks[3 + h], terms[D - 1][:, a:z], False, True)
+            per_own_gain(ratio[:, a:z], banks[3 + h], a)
+            add_turned(banks[5 + h], ratio[:, a:z], True, True)
+        weighted = heard_last(1, banks[1])
+        add_turned(banks[2], weighted[:], True, False)
+        for d in range(D - 1):
+            term = sb([P, S], F32, f"term1{d}")
+            gather(first[1], d, 0, S, term[:])
+            add_turned(banks[4], term[:], d == 0, d == D - 2)
+        ratio = sb([P, S], F32, "ratio1")
+        per_own_gain(ratio[:], banks[4], 0)
+        add_turned(banks[2], ratio[:], False, True)
+        for h, (a, z) in enumerate(halves):
+            limit(0, banks[5 + h][:, :HALF], a, z)
+
+        pieces = [(0, 0, HALF), (0, HALF, S), (1, 0, HALF), (1, HALF, S - P)]
+        turned_banks = [banks[7], banks[7], banks[7], banks[1], banks[4]]
+        back_banks = [banks[3], banks[5], banks[6], banks[0], banks[3]]
+        tags = {2: "noisy0", 3: "noisy1"}
         for i, (b, a, z) in enumerate(pieces):
-            heard(power[b], f"t1{b}_{a}_", a, z, turned_banks[i % 2], D)
-            if i == 1:
-                signals.append(limit(1, banks[6], banks[1]))
-            if len(pending) == 2:
-                finish(*pending.pop(0))
-            pending.append((b, rate_logs(b, signals[b], a, z, turned_banks[i % 2], both_banks[i % 3]), a, z))
-        for job in pending:
-            finish(*job)
+            width = z - a
+            if (b, a) == (1, 0):
+                limit(1, banks[2][:], 0, S)
+            if a % HALF == 0:
+                terms = keep.tile([P, D, HALF], F32, name=f"terms{i}", tag=tags.get(i, f"terms{i}"), align_bytes=64)
+            for d in range(D):
+                term = terms[:, d, a % HALF : a % HALF + width]
+                gather(power[b], d, a, z, term)
+                add_turned(turned_banks[i], term, d == 0, d == D - 1)
+            noisy = sb([P, width], F32, f"noisy{i}")
+            per_own_gain(noisy[:], turned_banks[i], a)
+            add_turned(back_banks[i], noisy[:], True, True)
+            back = back_banks[i][:, :width]
+            logs = sb([P, 2 * width], F32, f"logs{i}")
+            total = sb([P, width], F32, f"total{i}")
+            nc.vector.tensor_tensor(total[:], back, power[b][:, a:z], ALU.add)
+            nc.scalar.activation(logs[:, :width], back, ACT.Ln)
+            nc.scalar.activation(logs[:, width:], total[:], ACT.Ln)
+            rate = sb([P, width], F32, f"rate{i}")
+            nc.vector.tensor_tensor(rate[:], logs[:, width:], logs[:, :width], ALU.subtract)
+            nc.sync.dma_start(out=out[b * P : (b + 1) * P, a:z], in_=rate[:])
+        a = S - P
+        pair = sb([P, 2, P], F32, "pair")
+        signal = sb([P, P], F32, "signal")
+        last_terms = [terms[:, d, P:] for d in range(D)]
+        nc.vector.tensor_tensor(signal[:], power[1][:, a:S], own_tail[:], ALU.mult)
+        gather(power[1], 0, a, S, last_terms[0])
+        gather(power[1], 1, a, S, last_terms[1])
+        nc.vector.scalar_tensor_tensor(pair[:, 0, :], last_terms[0], NOISE, last_terms[1], ALU.add, ALU.add)
+        nc.vector.tensor_tensor(pair[:, 1, :], pair[:, 0, :], signal[:], ALU.add)
+        gather(power[1], 2, a, S, last_terms[2])
+        both = sb([P, 2, P], F32, "both")
+        nc.vector.tensor_tensor(both[:], pair[:], last_terms[2].unsqueeze(1).to_broadcast([P, 2, P]), ALU.add)
+        logs = sb([P, 2, P], F32, "logs_tail")
+        nc.scalar.activation(logs[:], both[:], ACT.Ln)
+        rate = sb([P, P], F32, "rate_tail")
+        nc.vector.tensor_tensor(rate[:], logs[:, 1, :], logs[:, 0, :], ALU.subtract)
+        nc.sync.dma_start(out=out[P:, a:S], in_=rate[:])

@@ -53,7 +53,13 @@ def tile_picked_yfosch_rate_p_kernel(
         exponents = sb([P, WIDE], F32, "exponents")
         gains = [sb([P, S], F32, f"gains{d}") for d in range(D)]
         caps = sb([P, S], F32, "caps")
-        rows = sb([P, P], F32, "rows")
+        own_cols = sb([P, CHUNKS], F32, "own_cols")
+        gain_cols = sb([P, CHUNKS], F32, "gain_cols")
+
+        def load_columns(cols, row):
+            with nc.allow_non_contiguous_dma(reason="one value a partition and chunk"):
+                nc.sync.dma_start(out=cols[:], in_=row.rearrange("(c p) -> p c", p=P))
+
         ident = sb([P, P], F32, "ident")
         first = [sb([P, WINDOW], F32, f"first{b}") for b in range(BLOCKS)]
         power = [sb([P, WINDOW], F32, f"power{b}") for b in range(BLOCKS)]
@@ -69,9 +75,6 @@ def tile_picked_yfosch_rate_p_kernel(
             nc.sync.dma_start(out=w_raw[b][o][:], in_=k_rows.rearrange("(p t) m -> p t m", t=PACK))
 
         nc.vector.memset(table_scales[:].bitcast(I32), 0)
-        warm = sb([P, 1], F32, "warm")
-        nc.vector.memset(warm[:], 0.0)
-        nc.vector.memset(rows[:], 0.0)
         nc.vector.memset(exponents[:, S:], 0.0)
         nc.sync.dma_start(out=picked[:], in_=offs)
         load_words(0)
@@ -82,8 +85,6 @@ def tile_picked_yfosch_rate_p_kernel(
             )
         load_w(0, 0)
         load_w(0, 1)
-        nc.sync.dma_start(out=rows[GAIN_ROW : GAIN_ROW + CHUNKS, :], in_=gain[D - 1, 0].rearrange("(c n) -> c n", n=P))
-        nc.sync.dma_start(out=rows[OWN_ROW : OWN_ROW + CHUNKS, :], in_=owng[0].rearrange("(c n) -> c n", n=P))
         load_words(1)
         nc.sync.dma_start(out=places[0][:], in_=pos1)
         nc.sync.dma_start(out=places[1][:], in_=pos2)
@@ -91,8 +92,10 @@ def tile_picked_yfosch_rate_p_kernel(
         load_w(1, 0)
         load_w(1, 1)
         nc.sync.dma_start(out=gains[0][:], in_=gain[0])
+        load_columns(own_cols, owng[0])
         nc.sync.dma_start(out=gains[1][:], in_=gain[1])
         nc.sync.dma_start(out=gains[2][:], in_=gain[2])
+        load_columns(gain_cols, gain[D - 1, 0])
         nc.sync.dma_start(out=caps[:], in_=cap)
         own_tail = sb([P, P], F32, "own_tail")
         nc.sync.dma_start(out=own_tail[:], in_=owng[:, S - P :])
@@ -104,8 +107,6 @@ def tile_picked_yfosch_rate_p_kernel(
         for window in first + power:
             nc.gpsimd.memset(window[:, S:], 0.0)
 
-        warm2 = sb([P, 1], F32, "warm2")
-        nc.scalar.activation(warm2[:], warm[:], ACT.Exp)
 
         scales = sb([P, S], U8, "scales")
         words = [sb([P, S], U32, f"words{o}") for o in range(PASSES)]
@@ -148,15 +149,6 @@ def tile_picked_yfosch_rate_p_kernel(
         cast_w(nc.scalar.copy, 0, 0)
         cast_w(nc.scalar.copy, 0, 1)
         quantize_w(0)
-        turn(banks[6][:, :P], rows[:], True, True)
-        cols = sb([P, ROWS], F32, "cols")
-        inv_own = sb([P, CHUNKS], F32, "inv_own")
-        floor = sb([P, CHUNKS], F32, "floor")
-        last_gain = sb([P, CHUNKS], F32, "last_gain")
-        nc.scalar.copy(cols[:], banks[6][:, :ROWS])
-        nc.vector.reciprocal(inv_own[:], cols[:, OWN_ROW : OWN_ROW + CHUNKS])
-        nc.gpsimd.tensor_scalar_mul(floor[:], inv_own[:], NOISE)
-        nc.gpsimd.tensor_tensor(last_gain[:], inv_own[:], cols[:, GAIN_ROW : GAIN_ROW + CHUNKS], ALU.mult)
         spans = [(0, HALF), (HALF, HALF + P), (HALF + P, S)]
         span_banks = [banks[0], banks[1], banks[7]]
         for bank, (a, z) in zip(span_banks, spans):
@@ -170,6 +162,14 @@ def tile_picked_yfosch_rate_p_kernel(
         quantize_w(1)
         product(banks[2][:], 1, 0, 0, S)
         product(banks[2][:], 1, 1, 0, S)
+        inv_own = sb([P, CHUNKS], F32, "inv_own")
+        floor = sb([P, CHUNKS], F32, "floor")
+        last_gain = sb([P, CHUNKS], F32, "last_gain")
+        nc.vector.reciprocal(inv_own[:], own_cols[:])
+        nc.scalar.activation(floor[:], inv_own[:], ACT.Copy, scale=NOISE)
+        nc.vector.tensor_tensor(last_gain[:], inv_own[:], gain_cols[:], ALU.mult)
+
+
         def gather(window, d, a, z, term):
             index = places[d][:] if z - a == S else places[d][:, entries(a, z)]
             nc.vector.tensor_tensor(term, window[:].indirect(index), gains[d][:, a:z], ALU.mult)
@@ -189,12 +189,12 @@ def tile_picked_yfosch_rate_p_kernel(
         def limit(b, back, a, z):
             nc.vector.scalar_tensor_tensor(power[b][:, a:z], back, goals[:, b : b + 1], caps[:, a:z], ALU.mult, ALU.min)
 
-        def heard_last(b, turned):
+        def heard_last(b, turned, after):
             last = sb([P, S], F32, f"last{b}")
             nc.scalar.activation(last[:], exponents[:].indirect(places[D - 1][:]), ACT.Exp, scale=0.4)
             if b == 1:
                 warm3 = sb([P, 1], F32, "warm3")
-                nc.scalar.activation(warm3[:], last[:, 0:1], ACT.Ln)
+                nc.scalar.activation(warm3[:], last[:, 0:1], ACT.Ln, bias=after)
             add_turned(turned, last[:], True, True)
             weighted = sb([P, S], F32, f"weighted{b}")
             for c in range(CHUNKS):
@@ -215,7 +215,7 @@ def tile_picked_yfosch_rate_p_kernel(
             add_turned(banks[3 + h], terms[D - 1][:, a:z], False, True)
             per_own_gain(ratio[:, a:z], banks[3 + h], a)
             add_turned(banks[5 + h], ratio[:, a:z], True, True)
-        weighted = heard_last(1, banks[1])
+        weighted = heard_last(1, banks[1], ratio[:, S - 1 : S])
         add_turned(banks[2], weighted[:], True, False)
         for d in range(D - 1):
             term = sb([P, S], F32, f"term1{d}")

@@ -22,12 +22,14 @@ PASSES = K // (P * PACK)
 BLOCKS = N // P
 CHUNKS = S // P
 HALF = S // 2
-LIST = 16
-WINDOW = S + 16
+QUADRANT = 32
+SCALE_ROWS = 4
+GROUP = 16
+WINDOW = S + GROUP
+EXP_WINDOW = 4 * S
+TAIL = S - P
+RATE = 0.4
 NOISE = 0.1
-OWN_ROW, GAIN_ROW, ROWS = 0, 4, 8
-WIDE = 2048
-OFFLOAD = (1,)
 
 
 def tile_picked_yfosch_rate_p_kernel(
@@ -39,30 +41,31 @@ def tile_picked_yfosch_rate_p_kernel(
         keep = ctx.enter_context(tc.tile_pool(name="keep", bufs=1))
         psum = ctx.enter_context(tc.psum_pool(name="psum", bufs=1))
 
-        def sb(shape, dtype, name):
-            return keep.tile(shape, dtype, name=name, align_bytes=64)
+        def sb(shape, dtype, name, tag=None):
+            return keep.tile(shape, dtype, name=name, tag=tag or name, align_bytes=64)
+
+        def entries(a, z):
+            return slice(a // GROUP, z // GROUP)
+
+        def chunk(c):
+            return slice(c * P, (c + 1) * P)
 
         banks = [psum.tile([P, S], F32, name=f"bank{i}") for i in range(8)]
 
-        picked = lists.tile([P, S // LIST], U16, name="picked")
-        places = [lists.tile([P, S // LIST], U16, name=f"places{d}") for d in range(D)]
+        picked = lists.tile([P, S // GROUP], U16, name="picked")
+        places = [lists.tile([P, S // GROUP], U16, name=f"places{d}") for d in range(D)]
 
         table_scales = sb([P, T], U8, "table_scales")
         table_words = [sb([P, T], U32, f"table_words{o}") for o in range(PASSES)]
         w_raw = [[sb([P, PACK, P], F32, f"w_raw{b}{o}") for o in range(PASSES)] for b in range(BLOCKS)]
-        exponents = sb([P, WIDE], F32, "exponents")
+        y1_window = sb([P, EXP_WINDOW], F32, "y1_window")
         gains = [sb([P, S], F32, f"gains{d}") for d in range(D)]
         caps = sb([P, S], F32, "caps")
-        own_cols = sb([P, CHUNKS], F32, "own_cols")
-        gain_cols = sb([P, CHUNKS], F32, "gain_cols")
-
-        def load_columns(cols, row):
-            with nc.allow_non_contiguous_dma(reason="one value a partition and chunk"):
-                nc.sync.dma_start(out=cols[:], in_=row.rearrange("(c p) -> p c", p=P))
-
+        own_turned = sb([P, CHUNKS], F32, "own_turned")
+        last_gain_turned = sb([P, CHUNKS], F32, "last_gain_turned")
         ident = sb([P, P], F32, "ident")
-        first = [sb([P, WINDOW], F32, f"first{b}") for b in range(BLOCKS)]
-        power = [sb([P, WINDOW], F32, f"power{b}") for b in range(BLOCKS)]
+        pw = [sb([P, WINDOW], F32, f"pw{b}") for b in range(BLOCKS)]
+        pn = [sb([P, WINDOW], F32, f"pn{b}") for b in range(BLOCKS)]
 
         def load_words(o):
             nc.sync.dma_start(
@@ -71,42 +74,49 @@ def tile_picked_yfosch_rate_p_kernel(
             )
 
         def load_w(b, o):
-            k_rows = w1[o * P * PACK : (o + 1) * P * PACK, b * P : (b + 1) * P]
+            k_rows = w1[o * P * PACK : (o + 1) * P * PACK, chunk(b)]
             nc.sync.dma_start(out=w_raw[b][o][:], in_=k_rows.rearrange("(p t) m -> p t m", t=PACK))
 
+        def load_turned(tile, values):
+            with nc.allow_non_contiguous_dma(reason="one value a partition and chunk"):
+                nc.sync.dma_start(out=tile[:], in_=values.rearrange("(c p) -> p c", p=P))
+
         nc.vector.memset(table_scales[:].bitcast(I32), 0)
-        nc.vector.memset(exponents[:, S:], 0.0)
+        exp_warm_in = sb([P, 1], F32, "exp_warm_in")
+        nc.vector.memset(exp_warm_in[:], 0.0)
+        nc.vector.memset(y1_window[:, S:], 0.0)
+
         nc.sync.dma_start(out=picked[:], in_=offs)
         load_words(0)
-        for q in range(4):
+        for q in range(P // QUADRANT):
             nc.sync.dma_start(
-                out=table_scales[32 * q : 32 * q + 8, :].bitcast(I32),
-                in_=x_scales[:, 4 * q : 4 * q + 4, :].bitcast(I32),
+                out=table_scales[QUADRANT * q : QUADRANT * q + PASSES * SCALE_ROWS, :].bitcast(I32),
+                in_=x_scales[:, SCALE_ROWS * q : SCALE_ROWS * (q + 1), :].bitcast(I32),
             )
         load_w(0, 0)
         load_w(0, 1)
         load_words(1)
-        nc.sync.dma_start(out=places[0][:], in_=pos1)
-        nc.sync.dma_start(out=places[1][:], in_=pos2)
-        nc.sync.dma_start(out=places[2][:], in_=pos3)
         load_w(1, 0)
+        for place, pos in zip(places, (pos1, pos2, pos3)):
+            nc.sync.dma_start(out=place[:], in_=pos)
         load_w(1, 1)
         nc.sync.dma_start(out=gains[0][:], in_=gain[0])
-        load_columns(own_cols, owng[0])
+        load_turned(own_turned, owng[0])
         nc.sync.dma_start(out=gains[1][:], in_=gain[1])
         nc.sync.dma_start(out=gains[2][:], in_=gain[2])
-        load_columns(gain_cols, gain[D - 1, 0])
+        load_turned(last_gain_turned, gain[D - 1, 0])
         nc.sync.dma_start(out=caps[:], in_=cap)
         own_tail = sb([P, P], F32, "own_tail")
-        nc.sync.dma_start(out=own_tail[:], in_=owng[:, S - P :])
+        nc.sync.dma_start(out=own_tail[:], in_=owng[:, TAIL:])
         goals = sb([P, BLOCKS], F32, "goals")
-        with nc.allow_non_contiguous_dma(reason="one goal a partition and block"):
-            nc.sync.dma_start(out=goals[:], in_=goal.rearrange("(b p) o -> p (b o)", p=P))
+        load_turned(goals, goal.rearrange("n o -> (n o)"))
 
         make_identity(nc, ident[:])
-        for window in first + power:
+        for window in pw + pn:
             nc.gpsimd.memset(window[:, S:], 0.0)
 
+        exp_warm_out = sb([P, 1], F32, "exp_warm_out")
+        nc.scalar.activation(exp_warm_out[:], exp_warm_in[:], ACT.Exp)
 
         scales = sb([P, S], U8, "scales")
         words = [sb([P, S], U32, f"words{o}") for o in range(PASSES)]
@@ -114,13 +124,7 @@ def tile_picked_yfosch_rate_p_kernel(
         w_codes = [sb([P, PASSES, P], U32, f"w_codes{b}") for b in range(BLOCKS)]
         w_scales = [sb([P, PASSES, P], U8, f"w_scales{b}") for b in range(BLOCKS)]
 
-        def entries(a, z):
-            return slice(a // LIST, z // LIST)
-
-        def chunk(c):
-            return slice(c * P, (c + 1) * P)
-
-        def cast_w(copy, b, o):
+        def round_w(copy, b, o):
             copy(w_bf[b][:, o], w_raw[b][o][:].rearrange("p t m -> p m t"))
 
         def quantize_w(b):
@@ -136,137 +140,149 @@ def tile_picked_yfosch_rate_p_kernel(
                 lhsT=w_codes[b][:, o].bitcast(FP8X4),
                 lhsT_scale=w_scales[b][:, o],
                 rhs=words[o][:, a:z].bitcast(FP8X4),
-                rhs_scale=scales[4 * o :, a:z],
+                rhs_scale=scales[SCALE_ROWS * o :, a:z],
                 start=(o == 0),
                 stop=(o == PASSES - 1),
             )
 
-        def turn(dst, src, start, stop):
-            nc.tensor.matmul(dst, lhsT=src, rhs=ident[:], is_transpose=True, start=start, stop=stop)
-
         nc.vector.tensor_copy(words[0][:], table_words[0][:].indirect(picked[:]))
         nc.vector.tensor_copy(scales[:], table_scales[:].indirect(picked[:]))
-        cast_w(nc.scalar.copy, 0, 0)
-        cast_w(nc.scalar.copy, 0, 1)
+        round_w(nc.scalar.copy, 0, 0)
+        round_w(nc.scalar.copy, 0, 1)
         quantize_w(0)
+        round_w(nc.scalar.copy, 1, 0)
         spans = [(0, HALF), (HALF, HALF + P), (HALF + P, S)]
-        span_banks = [banks[0], banks[1], banks[7]]
-        for bank, (a, z) in zip(span_banks, spans):
+        y0_banks = [banks[0], banks[1], banks[7]]
+        y1_bank = banks[2]
+        for bank, (a, z) in zip(y0_banks, spans):
             product(bank[:, : z - a], 0, 0, a, z)
-        for bank, (a, z) in zip(span_banks, spans):
+        for bank, (a, z) in zip(y0_banks, spans):
             nc.vector.tensor_copy(words[1][:, a:z], table_words[1][:].indirect(picked[:, entries(a, z)]))
             product(bank[:, : z - a], 0, 1, a, z)
-            nc.scalar.activation(first[0][:, a:z], bank[:, : z - a], ACT.Exp, scale=0.4)
-        cast_w(nc.vector.tensor_copy, 1, 0)
-        cast_w(nc.vector.tensor_copy, 1, 1)
+            nc.scalar.activation(pw[0][:, a:z], bank[:, : z - a], ACT.Exp, scale=RATE)
+        round_w(nc.vector.tensor_copy, 1, 1)
         quantize_w(1)
-        product(banks[2][:], 1, 0, 0, S)
-        product(banks[2][:], 1, 1, 0, S)
-        inv_own = sb([P, CHUNKS], F32, "inv_own")
-        floor = sb([P, CHUNKS], F32, "floor")
-        last_gain = sb([P, CHUNKS], F32, "last_gain")
-        nc.vector.reciprocal(inv_own[:], own_cols[:])
-        nc.scalar.activation(floor[:], inv_own[:], ACT.Copy, scale=NOISE)
-        nc.vector.tensor_tensor(last_gain[:], inv_own[:], gain_cols[:], ALU.mult)
+        for o in range(PASSES):
+            product(y1_bank[:], 1, o, 0, S)
 
+        inv_own = sb([P, CHUNKS], F32, "inv_own")
+        noise_per_own = sb([P, CHUNKS], F32, "noise_per_own")
+        last_gain_per_own = sb([P, CHUNKS], F32, "last_gain_per_own")
+        nc.vector.reciprocal(inv_own[:], own_turned[:])
+        nc.scalar.activation(noise_per_own[:], inv_own[:], ACT.Copy, scale=NOISE)
+        nc.vector.tensor_tensor(last_gain_per_own[:], inv_own[:], last_gain_turned[:], ALU.mult)
 
         def gather(window, d, a, z, term):
             index = places[d][:] if z - a == S else places[d][:, entries(a, z)]
             nc.vector.tensor_tensor(term, window[:].indirect(index), gains[d][:, a:z], ALU.mult)
 
-        def add_turned(turned, term, start, stop):
-            count = term.shape[1] // P
+        def add_turned(bank, values, start, stop):
+            count = values.shape[1] // P
             for c in range(count):
-                turn(turned[:, chunk(c)], term[:, chunk(c)], start and c == 0, stop and c == count - 1)
+                nc.tensor.matmul(
+                    bank[:, chunk(c)],
+                    lhsT=values[:, chunk(c)],
+                    rhs=ident[:],
+                    is_transpose=True,
+                    start=start and c == 0,
+                    stop=stop and c == count - 1,
+                )
 
         def per_own_gain(ratio, turned, a):
             for c in range(ratio.shape[1] // P):
-                link = slice(a // P + c, a // P + c + 1)
+                column = slice(a // P + c, a // P + c + 1)
                 nc.scalar.activation(
-                    ratio[:, chunk(c)], turned[:, chunk(c)], ACT.Identity, scale=inv_own[:, link], bias=floor[:, link]
+                    ratio[:, chunk(c)],
+                    turned[:, chunk(c)],
+                    ACT.Identity,
+                    scale=inv_own[:, column],
+                    bias=noise_per_own[:, column],
                 )
 
-        def limit(b, back, a, z):
-            nc.vector.scalar_tensor_tensor(power[b][:, a:z], back, goals[:, b : b + 1], caps[:, a:z], ALU.mult, ALU.min)
-
-        def heard_last(b, turned, after):
-            last = sb([P, S], F32, f"last{b}")
-            nc.scalar.activation(last[:], exponents[:].indirect(places[D - 1][:]), ACT.Exp, scale=0.4)
-            if b == 1:
-                warm3 = sb([P, 1], F32, "warm3")
-                nc.scalar.activation(warm3[:], last[:, 0:1], ACT.Ln, bias=after)
-            add_turned(turned, last[:], True, True)
-            weighted = sb([P, S], F32, f"weighted{b}")
-            for c in range(CHUNKS):
-                nc.scalar.activation(weighted[:, chunk(c)], turned[:, chunk(c)], ACT.Copy, scale=last_gain[:, c : c + 1])
-            return weighted
+        def set_power(b, ratio_bank, a, z):
+            nc.vector.scalar_tensor_tensor(
+                pn[b][:, a:z], ratio_bank, goals[:, b : b + 1], caps[:, a:z], ALU.mult, ALU.min
+            )
 
         halves = [(0, HALF), (HALF, S)]
-        ratio = sb([P, S], F32, "ratio0")
-        nc.scalar.activation(first[1][:, :S], banks[2][:], ACT.Exp, scale=0.4)
-        nc.scalar.copy(exponents[:, :S], banks[2][:])
-        terms = [sb([P, S], F32, f"term0{d}") for d in range(D)]
+        ia0_turned = [banks[3], banks[4]]
+        ia0_back = [banks[5], banks[6]]
+        ratio0 = sb([P, S], F32, "ratio0")
+        nc.scalar.activation(pw[1][:, :S], y1_bank[:], ACT.Exp, scale=RATE)
+        nc.scalar.copy(y1_window[:, :S], y1_bank[:])
+        ia0_terms = [sb([P, S], F32, f"ia0_term{d}") for d in range(D)]
         for d in range(D - 1):
-            gather(first[0], d, 0, S, terms[d][:])
-            for h, (a, z) in enumerate(halves):
-                add_turned(banks[3 + h], terms[d][:, a:z], d == 0, False)
-        for h, (a, z) in enumerate(halves):
-            gather(first[0], D - 1, a, z, terms[D - 1][:, a:z])
-            add_turned(banks[3 + h], terms[D - 1][:, a:z], False, True)
-            per_own_gain(ratio[:, a:z], banks[3 + h], a)
-            add_turned(banks[5 + h], ratio[:, a:z], True, True)
-        weighted = heard_last(1, banks[1], ratio[:, S - 1 : S])
-        add_turned(banks[2], weighted[:], True, False)
-        for d in range(D - 1):
-            term = sb([P, S], F32, f"term1{d}")
-            gather(first[1], d, 0, S, term[:])
-            add_turned(banks[4], term[:], d == 0, d == D - 2)
-        ratio = sb([P, S], F32, "ratio1")
-        per_own_gain(ratio[:], banks[4], 0)
-        add_turned(banks[2], ratio[:], False, True)
-        for h, (a, z) in enumerate(halves):
-            limit(0, banks[5 + h][:, :HALF], a, z)
+            gather(pw[0], d, 0, S, ia0_terms[d][:])
+            for turned, (a, z) in zip(ia0_turned, halves):
+                add_turned(turned, ia0_terms[d][:, a:z], d == 0, False)
+        for turned, back, (a, z) in zip(ia0_turned, ia0_back, halves):
+            gather(pw[0], D - 1, a, z, ia0_terms[D - 1][:, a:z])
+            add_turned(turned, ia0_terms[D - 1][:, a:z], False, True)
+            per_own_gain(ratio0[:, a:z], turned, a)
+            add_turned(back, ratio0[:, a:z], True, True)
 
-        pieces = [(0, 0, HALF), (0, HALF, S), (1, 0, HALF), (1, HALF, S - P)]
-        turned_banks = [banks[7], banks[7], banks[7], banks[1], banks[4]]
-        back_banks = [banks[3], banks[5], banks[6], banks[0], banks[3]]
-        tags = {2: "noisy0", 3: "noisy1"}
-        for i, (b, a, z) in enumerate(pieces):
+        last_turned, ia1_turned, ia1_back = banks[1], banks[4], y1_bank
+        last = sb([P, S], F32, "last")
+        nc.scalar.activation(last[:], y1_window[:].indirect(places[D - 1][:]), ACT.Exp, scale=RATE)
+        ln_warm = sb([P, 1], F32, "ln_warm")
+        nc.scalar.activation(ln_warm[:], last[:, 0:1], ACT.Ln, bias=ratio0[:, S - 1 : S])
+        add_turned(last_turned, last[:], True, True)
+        weighted = sb([P, S], F32, "weighted")
+        for c in range(CHUNKS):
+            nc.scalar.activation(
+                weighted[:, chunk(c)], last_turned[:, chunk(c)], ACT.Copy, scale=last_gain_per_own[:, c : c + 1]
+            )
+        add_turned(ia1_back, weighted[:], True, False)
+        for d in range(D - 1):
+            ia1_term = sb([P, S], F32, f"ia1_term{d}")
+            gather(pw[1], d, 0, S, ia1_term[:])
+            add_turned(ia1_turned, ia1_term[:], d == 0, d == D - 2)
+        ratio1 = sb([P, S], F32, "ratio1")
+        per_own_gain(ratio1[:], ia1_turned, 0)
+        add_turned(ia1_back, ratio1[:], False, True)
+        for back, (a, z) in zip(ia0_back, halves):
+            set_power(0, back[:, :HALF], a, z)
+
+        def store_rate(b, a, z, log_sum, log_heard):
+            rate = sb([P, z - a], F32, f"rate{b}_{a}")
+            nc.vector.tensor_tensor(rate[:], log_sum, log_heard, ALU.subtract)
+            nc.sync.dma_start(out=out[chunk(b), a:z], in_=rate[:])
+
+        def rates(b, a, z, terms, turned, back_bank):
             width = z - a
-            if (b, a) == (1, 0):
-                limit(1, banks[2][:], 0, S)
-            if a % HALF == 0:
-                terms = keep.tile([P, D, HALF], F32, name=f"terms{i}", tag=tags.get(i, f"terms{i}"), align_bytes=64)
             for d in range(D):
-                term = terms[:, d, a % HALF : a % HALF + width]
-                gather(power[b], d, a, z, term)
-                add_turned(turned_banks[i], term, d == 0, d == D - 1)
-            noisy = sb([P, width], F32, f"noisy{i}")
-            per_own_gain(noisy[:], turned_banks[i], a)
-            add_turned(back_banks[i], noisy[:], True, True)
-            back = back_banks[i][:, :width]
-            logs = sb([P, 2 * width], F32, f"logs{i}")
-            total = sb([P, width], F32, f"total{i}")
-            nc.vector.tensor_tensor(total[:], back, power[b][:, a:z], ALU.add)
+                gather(pn[b], d, a, z, terms[:, d, :])
+                add_turned(turned, terms[:, d, :], d == 0, d == D - 1)
+            heard = sb([P, width], F32, f"heard{b}_{a}")
+            per_own_gain(heard[:], turned, a)
+            add_turned(back_bank, heard[:], True, True)
+            back = back_bank[:, :width]
+            logs = sb([P, 2 * width], F32, f"logs{b}_{a}")
+            total = sb([P, width], F32, f"total{b}_{a}")
+            nc.vector.tensor_tensor(total[:], back, pn[b][:, a:z], ALU.add)
             nc.scalar.activation(logs[:, :width], back, ACT.Ln)
             nc.scalar.activation(logs[:, width:], total[:], ACT.Ln)
-            rate = sb([P, width], F32, f"rate{i}")
-            nc.vector.tensor_tensor(rate[:], logs[:, width:], logs[:, :width], ALU.subtract)
-            nc.sync.dma_start(out=out[b * P : (b + 1) * P, a:z], in_=rate[:])
-        a = S - P
+            store_rate(b, a, z, logs[:, width:], logs[:, :width])
+
+        ib_turned = banks[7]
+        for (a, z), back_bank in zip(halves, (banks[3], banks[5])):
+            rates(0, a, z, sb([P, D, HALF], F32, f"ib_terms0_{a}")[:], ib_turned, back_bank)
+        set_power(1, ia1_back[:], 0, S)
+        rates(1, 0, HALF, sb([P, D, HALF], F32, "ib_terms1_0", tag="heard0_0")[:], ib_turned, banks[6])
+        last_half = sb([P, D, HALF], F32, f"ib_terms1_{HALF}", tag=f"heard0_{HALF}")
+        rates(1, HALF, TAIL, last_half[:, :, :P], banks[1], banks[0])
+
         pair = sb([P, 2, P], F32, "pair")
         signal = sb([P, P], F32, "signal")
-        last_terms = [terms[:, d, P:] for d in range(D)]
-        nc.vector.tensor_tensor(signal[:], power[1][:, a:S], own_tail[:], ALU.mult)
-        gather(power[1], 0, a, S, last_terms[0])
-        gather(power[1], 1, a, S, last_terms[1])
-        nc.vector.scalar_tensor_tensor(pair[:, 0, :], last_terms[0], NOISE, last_terms[1], ALU.add, ALU.add)
+        tail_terms = [last_half[:, d, P:] for d in range(D)]
+        nc.vector.tensor_tensor(signal[:], pn[1][:, TAIL:S], own_tail[:], ALU.mult)
+        gather(pn[1], 0, TAIL, S, tail_terms[0])
+        gather(pn[1], 1, TAIL, S, tail_terms[1])
+        nc.vector.scalar_tensor_tensor(pair[:, 0, :], tail_terms[0], NOISE, tail_terms[1], ALU.add, ALU.add)
         nc.vector.tensor_tensor(pair[:, 1, :], pair[:, 0, :], signal[:], ALU.add)
-        gather(power[1], 2, a, S, last_terms[2])
-        both = sb([P, 2, P], F32, "both")
-        nc.vector.tensor_tensor(both[:], pair[:], last_terms[2].unsqueeze(1).to_broadcast([P, 2, P]), ALU.add)
-        logs = sb([P, 2, P], F32, "logs_tail")
-        nc.scalar.activation(logs[:], both[:], ACT.Ln)
-        rate = sb([P, P], F32, "rate_tail")
-        nc.vector.tensor_tensor(rate[:], logs[:, 1, :], logs[:, 0, :], ALU.subtract)
-        nc.sync.dma_start(out=out[P:, a:S], in_=rate[:])
+        gather(pn[1], 2, TAIL, S, tail_terms[2])
+        whole_pair = sb([P, 2, P], F32, "whole_pair")
+        nc.vector.tensor_tensor(whole_pair[:], pair[:], tail_terms[2].unsqueeze(1).to_broadcast([P, 2, P]), ALU.add)
+        tail_logs = sb([P, 2, P], F32, "tail_logs")
+        nc.scalar.activation(tail_logs[:], whole_pair[:], ACT.Ln)
+        store_rate(1, TAIL, S, tail_logs[:, 1, :], tail_logs[:, 0, :])

@@ -61,8 +61,7 @@ def tile_picked_yfosch_rate_p_kernel(
         y1_window = sb([P, EXP_WINDOW], F32, "y1_window")
         gains = [sb([P, S], F32, f"gains{d}") for d in range(D)]
         caps = sb([P, S], F32, "caps")
-        own_turned = sb([P, CHUNKS], F32, "own_turned")
-        last_gain_turned = sb([P, CHUNKS], F32, "last_gain_turned")
+        link_rows = sb([P, P], F32, "link_rows")
         ident = sb([P, P], F32, "ident")
         pw = [sb([P, WINDOW], F32, f"pw{b}") for b in range(BLOCKS)]
         pn = [sb([P, WINDOW], F32, f"pn{b}") for b in range(BLOCKS)]
@@ -77,13 +76,10 @@ def tile_picked_yfosch_rate_p_kernel(
             k_rows = w1[o * P * PACK : (o + 1) * P * PACK, chunk(b)]
             nc.sync.dma_start(out=w_raw[b][o][:], in_=k_rows.rearrange("(p t) m -> p t m", t=PACK))
 
-        def load_turned(tile, values):
-            with nc.allow_non_contiguous_dma(reason="one value a partition and chunk"):
-                nc.sync.dma_start(out=tile[:], in_=values.rearrange("(c p) -> p c", p=P))
-
         nc.vector.memset(table_scales[:].bitcast(I32), 0)
         exp_warm_in = sb([P, 1], F32, "exp_warm_in")
         nc.vector.memset(exp_warm_in[:], 0.0)
+        nc.vector.memset(link_rows[:], 0.0)
         nc.vector.memset(y1_window[:, S:], 0.0)
 
         nc.sync.dma_start(out=picked[:], in_=offs)
@@ -97,19 +93,20 @@ def tile_picked_yfosch_rate_p_kernel(
         load_w(0, 1)
         load_words(1)
         load_w(1, 0)
+        for i, row in enumerate((owng[0], gain[D - 1, 0])):
+            nc.sync.dma_start(out=link_rows[CHUNKS * i : CHUNKS * (i + 1), :], in_=row.rearrange("(c n) -> c n", n=P))
         for place, pos in zip(places, (pos1, pos2, pos3)):
             nc.sync.dma_start(out=place[:], in_=pos)
         load_w(1, 1)
         nc.sync.dma_start(out=gains[0][:], in_=gain[0])
-        load_turned(own_turned, owng[0])
         nc.sync.dma_start(out=gains[1][:], in_=gain[1])
         nc.sync.dma_start(out=gains[2][:], in_=gain[2])
-        load_turned(last_gain_turned, gain[D - 1, 0])
         nc.sync.dma_start(out=caps[:], in_=cap)
         own_tail = sb([P, P], F32, "own_tail")
         nc.sync.dma_start(out=own_tail[:], in_=owng[:, TAIL:])
         goals = sb([P, BLOCKS], F32, "goals")
-        load_turned(goals, goal.rearrange("n o -> (n o)"))
+        with nc.allow_non_contiguous_dma(reason="one goal a partition and block"):
+            nc.sync.dma_start(out=goals[:], in_=goal.rearrange("(b p) o -> p (b o)", p=P))
 
         make_identity(nc, ident[:])
         for window in pw + pn:
@@ -165,13 +162,6 @@ def tile_picked_yfosch_rate_p_kernel(
         for o in range(PASSES):
             product(y1_bank[:], 1, o, 0, S)
 
-        inv_own = sb([P, CHUNKS], F32, "inv_own")
-        noise_per_own = sb([P, CHUNKS], F32, "noise_per_own")
-        last_gain_per_own = sb([P, CHUNKS], F32, "last_gain_per_own")
-        nc.vector.reciprocal(inv_own[:], own_turned[:])
-        nc.scalar.activation(noise_per_own[:], inv_own[:], ACT.Copy, scale=NOISE)
-        nc.vector.tensor_tensor(last_gain_per_own[:], inv_own[:], last_gain_turned[:], ALU.mult)
-
         def gather(window, d, a, z, term):
             index = places[d][:] if z - a == S else places[d][:, entries(a, z)]
             nc.vector.tensor_tensor(term, window[:].indirect(index), gains[d][:, a:z], ALU.mult)
@@ -187,6 +177,10 @@ def tile_picked_yfosch_rate_p_kernel(
                     start=start and c == 0,
                     stop=stop and c == count - 1,
                 )
+
+        link_cols = sb([P, 2 * CHUNKS], F32, "link_cols")
+        add_turned(banks[6], link_rows[:], True, True)
+        nc.scalar.copy(link_cols[:], banks[6][:, : 2 * CHUNKS])
 
         def per_own_gain(ratio, turned, a):
             for c in range(ratio.shape[1] // P):
@@ -215,6 +209,12 @@ def tile_picked_yfosch_rate_p_kernel(
             gather(pw[0], d, 0, S, ia0_terms[d][:])
             for turned, (a, z) in zip(ia0_turned, halves):
                 add_turned(turned, ia0_terms[d][:, a:z], d == 0, False)
+        inv_own = sb([P, CHUNKS], F32, "inv_own", tag="ia0_term0")
+        noise_per_own = sb([P, CHUNKS], F32, "noise_per_own")
+        last_gain_per_own = sb([P, CHUNKS], F32, "last_gain_per_own")
+        nc.vector.reciprocal(inv_own[:], link_cols[:, :CHUNKS])
+        nc.scalar.activation(noise_per_own[:], inv_own[:], ACT.Copy, scale=NOISE)
+        nc.vector.tensor_tensor(last_gain_per_own[:], inv_own[:], link_cols[:, CHUNKS:], ALU.mult)
         for turned, back, (a, z) in zip(ia0_turned, ia0_back, halves):
             gather(pw[0], D - 1, a, z, ia0_terms[D - 1][:, a:z])
             add_turned(turned, ia0_terms[D - 1][:, a:z], False, True)
@@ -224,8 +224,6 @@ def tile_picked_yfosch_rate_p_kernel(
         last_turned, ia1_turned, ia1_back = banks[1], banks[4], y1_bank
         last = sb([P, S], F32, "last")
         nc.scalar.activation(last[:], y1_window[:].indirect(places[D - 1][:]), ACT.Exp, scale=RATE)
-        ln_warm = sb([P, 1], F32, "ln_warm")
-        nc.scalar.activation(ln_warm[:], last[:, 0:1], ACT.Ln, bias=ratio0[:, S - 1 : S])
         add_turned(last_turned, last[:], True, True)
         weighted = sb([P, S], F32, "weighted")
         for c in range(CHUNKS):

from contextlib import ExitStack

import concourse.mybir as mybir
from concourse.masks import make_identity

K, T, S, N, D = 1024, 1024, 512, 256, 3
FLOPS = 2 * K * S * N

F32 = mybir.dt.float32
BF16 = mybir.dt.bfloat16
I32 = mybir.dt.int32
U32 = mybir.dt.uint32
U16 = mybir.dt.uint16
U8 = mybir.dt.uint8
FP8X4 = mybir.dt.float8_e4m3fn_x4
ACT = mybir.ActivationFunctionType
ALU = mybir.AluOpType

P = 128
PACK = 4
PASSES = K // (P * PACK)
BLOCKS = N // P
CHUNKS = S // P
HALF = S // 2
QUADRANT = 32
SCALE_ROWS = 4
GROUP = 16
WINDOW = S + GROUP
EXP_WINDOW = 4 * S
TAIL = S - P
RATE = 0.4
NOISE = 0.1


def tile_picked_yfosch_rate_p_kernel(
    tc, x_words, x_scales, w1, gain, owng, goal, cap, offs, pos1, pos2, pos3, out
):
    nc = tc.nc
    with ExitStack() as ctx:
        lists = ctx.enter_context(tc.tile_pool(name="lists", bufs=1))
        keep = ctx.enter_context(tc.tile_pool(name="keep", bufs=1))
        psum = ctx.enter_context(tc.psum_pool(name="psum", bufs=1))

        def sb(shape, dtype, name, tag=None):
            return keep.tile(shape, dtype, name=name, tag=tag or name, align_bytes=64)

        def entries(a, z):
            return slice(a // GROUP, z // GROUP)

        def chunk(c):
            return slice(c * P, (c + 1) * P)

        banks = [psum.tile([P, S], F32, name=f"bank{i}") for i in range(8)]

        picked = lists.tile([P, S // GROUP], U16, name="picked")
        places = [lists.tile([P, S // GROUP], U16, name=f"places{d}") for d in range(D)]

        table_scales = sb([P, T], U8, "table_scales")
        table_words = [sb([P, T], U32, f"table_words{o}") for o in range(PASSES)]
        w_raw = [[sb([P, PACK, P], F32, f"w_raw{b}{o}") for o in range(PASSES)] for b in range(BLOCKS)]
        y1_window = sb([P, EXP_WINDOW], F32, "y1_window")
        gains = [sb([P, S], F32, f"gains{d}") for d in range(D)]
        caps = sb([P, S], F32, "caps")
        link_rows = sb([P, P], F32, "link_rows")
        ident = sb([P, P], F32, "ident")
        pw = [sb([P, WINDOW], F32, f"pw{b}") for b in range(BLOCKS)]
        pn = [sb([P, WINDOW], F32, f"pn{b}") for b in range(BLOCKS)]

        def load_words(o):
            nc.sync.dma_start(
                out=table_words[o][:].bitcast(I32),
                in_=x_words[o].rearrange("p n t -> p (n t)").bitcast(I32),
            )

        def load_w(b, o):
            k_rows = w1[o * P * PACK : (o + 1) * P * PACK, chunk(b)]
            nc.sync.dma_start(out=w_raw[b][o][:], in_=k_rows.rearrange("(p t) m -> p t m", t=PACK))

        nc.vector.memset(table_scales[:].bitcast(I32), 0)
        exp_warm_in = sb([P, 1], F32, "exp_warm_in")
        nc.vector.memset(exp_warm_in[:], 0.0)
        nc.vector.memset(link_rows[:], 0.0)
        nc.vector.memset(y1_window[:, S:], 0.0)

        nc.sync.dma_start(out=picked[:], in_=offs)
        load_words(0)
        for q in range(P // QUADRANT):
            nc.sync.dma_start(
                out=table_scales[QUADRANT * q : QUADRANT * q + PASSES * SCALE_ROWS, :].bitcast(I32),
                in_=x_scales[:, SCALE_ROWS * q : SCALE_ROWS * (q + 1), :].bitcast(I32),
            )
        load_w(0, 0)
        load_w(0, 1)
        load_words(1)
        load_w(1, 0)
        for i, row in enumerate((owng[0], gain[D - 1, 0])):
            nc.sync.dma_start(out=link_rows[CHUNKS * i : CHUNKS * (i + 1), :], in_=row.rearrange("(c n) -> c n", n=P))
        for place, pos in zip(places, (pos1, pos2, pos3)):
            nc.sync.dma_start(out=place[:], in_=pos)
        load_w(1, 1)
        nc.sync.dma_start(out=gains[0][:], in_=gain[0])
        nc.sync.dma_start(out=gains[1][:], in_=gain[1])
        nc.sync.dma_start(out=gains[2][:], in_=gain[2])
        nc.sync.dma_start(out=caps[:], in_=cap)
        own_tail = sb([P, P], F32, "own_tail")
        nc.sync.dma_start(out=own_tail[:], in_=owng[:, TAIL:])
        goals = sb([P, BLOCKS], F32, "goals")
        with nc.allow_non_contiguous_dma(reason="one goal a partition and block"):
            nc.sync.dma_start(out=goals[:], in_=goal.rearrange("(b p) o -> p (b o)", p=P))

        make_identity(nc, ident[:])
        for window in pw + pn:
            nc.gpsimd.memset(window[:, S:], 0.0)

        exp_warm_out = sb([P, 1], F32, "exp_warm_out")
        nc.scalar.activation(exp_warm_out[:], exp_warm_in[:], ACT.Exp)

        scales = sb([P, S], U8, "scales")
        words = [sb([P, S], U32, f"words{o}") for o in range(PASSES)]
        w_bf = [sb([P, PASSES, P, PACK], BF16, f"w_bf{b}") for b in range(BLOCKS)]
        w_codes = [sb([P, PASSES, P], U32, f"w_codes{b}") for b in range(BLOCKS)]
        w_scales = [sb([P, PASSES, P], U8, f"w_scales{b}") for b in range(BLOCKS)]

        def round_w(copy, b, o):
            copy(w_bf[b][:, o], w_raw[b][o][:].rearrange("p t m -> p m t"))

        def quantize_w(b):
            nc.vector.quantize_mx(
                out=w_codes[b][:].rearrange("p o m -> p (o m)").bitcast(FP8X4),
                scales=w_scales[b][:].rearrange("p o m -> p (o m)"),
                in_=w_bf[b][:].rearrange("p o m t -> p (o m t)"),
            )

        def product(acc, b, o, a, z):
            nc.tensor.matmul_mx(
                out=acc,
                lhsT=w_codes[b][:, o].bitcast(FP8X4),
                lhsT_scale=w_scales[b][:, o],
                rhs=words[o][:, a:z].bitcast(FP8X4),
                rhs_scale=scales[SCALE_ROWS * o :, a:z],
                start=(o == 0),
                stop=(o == PASSES - 1),
            )

        nc.vector.tensor_copy(words[0][:], table_words[0][:].indirect(picked[:]))
        nc.vector.tensor_copy(scales[:], table_scales[:].indirect(picked[:]))
        round_w(nc.scalar.copy, 0, 0)
        round_w(nc.scalar.copy, 0, 1)
        quantize_w(0)
        round_w(nc.scalar.copy, 1, 0)
        spans = [(0, HALF), (HALF, HALF + P), (HALF + P, S)]
        y0_banks = [banks[0], banks[1], banks[7]]
        y1_bank = banks[2]
        for bank, (a, z) in zip(y0_banks, spans):
            product(bank[:, : z - a], 0, 0, a, z)
        for bank, (a, z) in zip(y0_banks, spans):
            nc.vector.tensor_copy(words[1][:, a:z], table_words[1][:].indirect(picked[:, entries(a, z)]))
            product(bank[:, : z - a], 0, 1, a, z)
            nc.scalar.activation(pw[0][:, a:z], bank[:, : z - a], ACT.Exp, scale=RATE)
        round_w(nc.vector.tensor_copy, 1, 1)
        quantize_w(1)
        for o in range(PASSES):
            product(y1_bank[:], 1, o, 0, S)

        def gather(window, d, a, z, term):
            index = places[d][:] if z - a == S else places[d][:, entries(a, z)]
            nc.vector.tensor_tensor(term, window[:].indirect(index), gains[d][:, a:z], ALU.mult)

        def add_turned(bank, values, start, stop):
            count = values.shape[1] // P
            for c in range(count):
                nc.tensor.matmul(
                    bank[:, chunk(c)],
                    lhsT=values[:, chunk(c)],
                    rhs=ident[:],
                    is_transpose=True,
                    start=start and c == 0,
                    stop=stop and c == count - 1,
                )

        link_cols = sb([P, 2 * CHUNKS], F32, "link_cols")
        add_turned(banks[6], link_rows[:], True, True)
        nc.scalar.copy(link_cols[:], banks[6][:, : 2 * CHUNKS])

        def per_own_gain(ratio, turned, a):
            for c in range(ratio.shape[1] // P):
                column = slice(a // P + c, a // P + c + 1)
                nc.scalar.activation(
                    ratio[:, chunk(c)],
                    turned[:, chunk(c)],
                    ACT.Identity,
                    scale=inv_own[:, column],
                    bias=noise_per_own[:, column],
                )

        def set_power(b, ratio_bank, a, z):
            nc.vector.scalar_tensor_tensor(
                pn[b][:, a:z], ratio_bank, goals[:, b : b + 1], caps[:, a:z], ALU.mult, ALU.min
            )

        halves = [(0, HALF), (HALF, S)]
        ia0_turned = [banks[3], banks[4]]
        ia0_back = [banks[5], banks[6]]
        ratio0 = sb([P, S], F32, "ratio0")
        nc.scalar.activation(pw[1][:, :S], y1_bank[:], ACT.Exp, scale=RATE)
        nc.scalar.copy(y1_window[:, :S], y1_bank[:])
        ia0_terms = [sb([P, S], F32, f"ia0_term{d}") for d in range(D)]
        for d in range(D - 1):
            gather(pw[0], d, 0, S, ia0_terms[d][:])
            for turned, (a, z) in zip(ia0_turned, halves):
                add_turned(turned, ia0_terms[d][:, a:z], d == 0, False)
        inv_own = sb([P, CHUNKS], F32, "inv_own", tag="ia0_term0")
        noise_per_own = sb([P, CHUNKS], F32, "noise_per_own")
        last_gain_per_own = sb([P, CHUNKS], F32, "last_gain_per_own")
        nc.vector.reciprocal(inv_own[:], link_cols[:, :CHUNKS])
        nc.scalar.activation(noise_per_own[:], inv_own[:], ACT.Copy, scale=NOISE)
        nc.vector.tensor_tensor(last_gain_per_own[:], inv_own[:], link_cols[:, CHUNKS:], ALU.mult)
        for turned, back, (a, z) in zip(ia0_turned, ia0_back, halves):
            gather(pw[0], D - 1, a, z, ia0_terms[D - 1][:, a:z])
            add_turned(turned, ia0_terms[D - 1][:, a:z], False, True)
            per_own_gain(ratio0[:, a:z], turned, a)
            add_turned(back, ratio0[:, a:z], True, True)

        last_turned, ia1_turned, ia1_back = banks[1], banks[4], y1_bank
        last = sb([P, S], F32, "last")
        nc.scalar.activation(last[:], y1_window[:].indirect(places[D - 1][:]), ACT.Exp, scale=RATE)
        add_turned(last_turned, last[:], True, True)
        weighted = sb([P, S], F32, "weighted")
        for c in range(CHUNKS):
            nc.scalar.activation(
                weighted[:, chunk(c)], last_turned[:, chunk(c)], ACT.Copy, scale=last_gain_per_own[:, c : c + 1]
            )
        add_turned(ia1_back, weighted[:], True, False)
        for d in range(D - 1):
            ia1_term = sb([P, S], F32, f"ia1_term{d}")
            gather(pw[1], d, 0, S, ia1_term[:])
            add_turned(ia1_turned, ia1_term[:], d == 0, d == D - 2)
        ratio1 = sb([P, S], F32, "ratio1")
        per_own_gain(ratio1[:], ia1_turned, 0)
        add_turned(ia1_back, ratio1[:], False, True)
        for back, (a, z) in zip(ia0_back, halves):
            set_power(0, back[:, :HALF], a, z)

        def store_rate(b, a, z, log_sum, log_heard):
            rate = sb([P, z - a], F32, f"rate{b}_{a}")
            nc.vector.tensor_tensor(rate[:], log_sum, log_heard, ALU.subtract)
            nc.sync.dma_start(out=out[chunk(b), a:z], in_=rate[:])

        def rates(b, a, z, terms, turned, back_bank):
            width = z - a
            for d in range(D):
                gather(pn[b], d, a, z, terms[:, d, :])
                add_turned(turned, terms[:, d, :], d == 0, d == D - 1)
            heard = sb([P, width], F32, f"heard{b}_{a}")
            per_own_gain(heard[:], turned, a)
            add_turned(back_bank, heard[:], True, True)
            back = back_bank[:, :width]
            logs = sb([P, 2 * width], F32, f"logs{b}_{a}")
            total = sb([P, width], F32, f"total{b}_{a}")
            nc.vector.tensor_tensor(total[:], back, pn[b][:, a:z], ALU.add)
            nc.scalar.activation(logs[:, :width], back, ACT.Ln)
            nc.scalar.activation(logs[:, width:], total[:], ACT.Ln)
            store_rate(b, a, z, logs[:, width:], logs[:, :width])

        ib_turned = banks[7]
        for (a, z), back_bank in zip(halves, (banks[3], banks[5])):
            rates(0, a, z, sb([P, D, HALF], F32, f"ib_terms0_{a}")[:], ib_turned, back_bank)
        set_power(1, ia1_back[:], 0, S)
        rates(1, 0, HALF, sb([P, D, HALF], F32, "ib_terms1_0", tag="heard0_0")[:], ib_turned, banks[6])
        last_half = sb([P, D, HALF], F32, f"ib_terms1_{HALF}", tag=f"heard0_{HALF}")
        rates(1, HALF, TAIL, last_half[:, :, :P], banks[1], banks[0])

        pair = sb([P, 2, P], F32, "pair")
        signal = sb([P, P], F32, "signal")
        tail_terms = [last_half[:, d, P:] for d in range(D)]
        nc.vector.tensor_tensor(signal[:], pn[1][:, TAIL:S], own_tail[:], ALU.mult)
        gather(pn[1], 0, TAIL, S, tail_terms[0])
        gather(pn[1], 1, TAIL, S, tail_terms[1])
        nc.vector.scalar_tensor_tensor(pair[:, 0, :], tail_terms[0], NOISE, tail_terms[1], ALU.add, ALU.add)
        nc.vector.tensor_tensor(pair[:, 1, :], pair[:, 0, :], signal[:], ALU.add)
        gather(pn[1], 2, TAIL, S, tail_terms[2])
        whole_pair = sb([P, 2, P], F32, "whole_pair")
        nc.vector.tensor_tensor(whole_pair[:], pair[:], tail_terms[2].unsqueeze(1).to_broadcast([P, 2, P]), ALU.add)
        tail_logs = sb([P, 2, P], F32, "tail_logs")
        nc.scalar.activation(tail_logs[:], whole_pair[:], ACT.Ln)
        store_rate(1, TAIL, S, tail_logs[:, 1, :], tail_logs[:, 0, :])
